import numpy as np
import ml_dtypes

BF16 = ml_dtypes.bfloat16


def bf(x):
    return np.asarray(x, np.float32).astype(BF16)


def f32(x):
    return np.asarray(x, np.float32)


def f64(x):
    return np.asarray(x).astype(np.float64)


def striped(idx):
    return np.tile(idx.reshape(-1, 16).T, (8, 1))


S, K, M, N = 4096, 256, 256, 1536


def setup_inputs():
    return {"table": bf(np.random.standard_normal((K, S))), "w": bf(np.random.standard_normal((K, M)) / np.sqrt(K)), "u": f32(np.random.standard_normal((M, N))), "offs": striped(np.random.permutation(S)[:N])}


def reference(table, w, u, offs):
    idx = offs[:16].T.reshape(-1)
    x = f64(table)[:, idx]
    y = f64(w).T @ x
    return y * f64(u)

@@ -1,0 +1,62 @@
+import concourse.mybir as mybir
+
+BF16, F32, U16 = mybir.dt.bfloat16, mybir.dt.float32, mybir.dt.uint16
+
+P = 128
+K, S, M, N = 256, 4096, 256, 1536
+K_BLOCKS = K // P
+M_BLOCKS = M // P
+PIECE = 512
+PIECES = N // PIECE
+PIECE_COLUMNS = PIECE // 16
+
+FLOPS = 2 * K * M * N
+
+
+def tile_gather_matmul_kernel(tc, table, w, u, offs, out):
+    nc = tc.nc
+    with (
+        tc.tile_pool(name="held", bufs=1) as held,
+        tc.psum_pool(name="psum", bufs=1) as psum,
+    ):
+        offsets = held.tile([P, N // 16], U16, name="offsets")
+        nc.sync.dma_start(offsets[:], offs)
+
+        table_blocks = []
+        weight_blocks = []
+        for kb in range(K_BLOCKS):
+            rows = slice(kb * P, (kb + 1) * P)
+            weight_block = held.tile([P, M], BF16, name="weights%d" % kb)
+            nc.scalar.dma_start(weight_block[:], w[rows, :])
+            weight_blocks.append(weight_block)
+            table_block = held.tile([P, S], BF16, name="table%d" % kb)
+            nc.sync.dma_start(table_block[:], table[rows, :])
+            table_blocks.append(table_block)
+
+        factor_blocks = []
+        for mb in range(M_BLOCKS):
+            factor_block = held.tile([P, N], F32, name="factor%d" % mb)
+            nc.scalar.dma_start(factor_block[:], u[mb * P : (mb + 1) * P, :])
+            factor_blocks.append(factor_block)
+
+        for mb in range(M_BLOCKS):
+            out_rows = slice(mb * P, (mb + 1) * P)
+            for piece in range(PIECES):
+                columns = slice(piece * PIECE, (piece + 1) * PIECE)
+                piece_offsets = offsets[:, piece * PIECE_COLUMNS : (piece + 1) * PIECE_COLUMNS]
+
+                bank = psum.tile([P, PIECE], F32, name="bank%d_%d" % (mb, piece))
+                for kb in range(K_BLOCKS):
+                    nc.tensor.matmul(
+                        bank[:],
+                        weight_blocks[kb][:, out_rows],
+                        table_blocks[kb][:].indirect(piece_offsets),
+                        start=(kb == 0),
+                        stop=(kb == K_BLOCKS - 1),
+                    )
+
+                product = held.tile([P, PIECE], F32, name="product%d_%d" % (mb, piece))
+                nc.vector.tensor_tensor(
+                    product[:], bank[:], factor_blocks[mb][:, columns], mybir.AluOpType.mult
+                )
+                nc.sync.dma_start(out[out_rows, columns], product[:])

@@ -21,42 +21,41 @@ def tile_gather_matmul_kernel(tc, table, w, u, offs, out):
     ):
         offsets = held.tile([P, N // 16], U16, name="offsets")
         nc.sync.dma_start(offsets[:], offs)
+        weights = held.tile([P, K_BLOCKS, M], BF16, name="weights")
+        nc.scalar.dma_start(weights[:], w.rearrange("(kb p) m -> p kb m", p=P))
 
         table_blocks = []
-        weight_blocks = []
         for kb in range(K_BLOCKS):
-            rows = slice(kb * P, (kb + 1) * P)
-            weight_block = held.tile([P, M], BF16, name="weights%d" % kb)
-            nc.scalar.dma_start(weight_block[:], w[rows, :])
-            weight_blocks.append(weight_block)
             table_block = held.tile([P, S], BF16, name="table%d" % kb)
-            nc.sync.dma_start(table_block[:], table[rows, :])
+            nc.sync.dma_start(table_block[:], table[kb * P : (kb + 1) * P, :])
             table_blocks.append(table_block)
-
         factor_blocks = []
         for mb in range(M_BLOCKS):
             factor_block = held.tile([P, N], F32, name="factor%d" % mb)
-            nc.scalar.dma_start(factor_block[:], u[mb * P : (mb + 1) * P, :])
+            nc.sync.dma_start(factor_block[:], u[mb * P : (mb + 1) * P, :])
             factor_blocks.append(factor_block)
 
-        for mb in range(M_BLOCKS):
-            out_rows = slice(mb * P, (mb + 1) * P)
-            for piece in range(PIECES):
-                columns = slice(piece * PIECE, (piece + 1) * PIECE)
-                piece_offsets = offsets[:, piece * PIECE_COLUMNS : (piece + 1) * PIECE_COLUMNS]
+        output_tiles = [(mb, piece) for mb in range(M_BLOCKS) for piece in range(PIECES)]
+        banks = {}
+        for mb, piece in output_tiles:
+            banks[mb, piece] = psum.tile([P, PIECE], F32, name="bank%d_%d" % (mb, piece))
 
-                bank = psum.tile([P, PIECE], F32, name="bank%d_%d" % (mb, piece))
-                for kb in range(K_BLOCKS):
-                    nc.tensor.matmul(
-                        bank[:],
-                        weight_blocks[kb][:, out_rows],
-                        table_blocks[kb][:].indirect(piece_offsets),
-                        start=(kb == 0),
-                        stop=(kb == K_BLOCKS - 1),
-                    )
-
-                product = held.tile([P, PIECE], F32, name="product%d_%d" % (mb, piece))
-                nc.vector.tensor_tensor(
-                    product[:], bank[:], factor_blocks[mb][:, columns], mybir.AluOpType.mult
+        for kb in range(K_BLOCKS):
+            for mb, piece in output_tiles:
+                nc.tensor.matmul(
+                    banks[mb, piece][:],
+                    weights[:, kb, mb * P : (mb + 1) * P],
+                    table_blocks[kb][:].indirect(
+                        offsets[:, piece * PIECE_COLUMNS : (piece + 1) * PIECE_COLUMNS]
+                    ),
+                    start=(kb == 0),
+                    stop=(kb == K_BLOCKS - 1),
                 )
-                nc.sync.dma_start(out[out_rows, columns], product[:])
+
+        for mb, piece in output_tiles:
+            columns = slice(piece * PIECE, (piece + 1) * PIECE)
+            product = held.tile([P, PIECE], F32, name="product%d_%d" % (mb, piece))
+            nc.vector.tensor_tensor(
+                product[:], banks[mb, piece][:], factor_blocks[mb][:, columns], mybir.AluOpType.mult
+            )
+            nc.scalar.dma_start(out[mb * P : (mb + 1) * P, columns], product[:])

@@ -10,6 +10,8 @@ PIECE = 512
 PIECES = N // PIECE
 PIECE_COLUMNS = PIECE // 16
 
+WARM_UPS = 7
+
 FLOPS = 2 * K * M * N
 
 
@@ -34,6 +36,12 @@ def tile_gather_matmul_kernel(tc, table, w, u, offs, out):
             factor_block = held.tile([P, N], F32, name="factor%d" % mb)
             nc.sync.dma_start(factor_block[:], u[mb * P : (mb + 1) * P, :])
             factor_blocks.append(factor_block)
+
+        zeros = held.tile([P, PIECE], BF16, name="zeros")
+        nc.vector.memset(zeros[:], 0.0)
+        warm_bank = psum.tile([P, PIECE], F32, name="warm_bank")
+        for warm_up in range(WARM_UPS):
+            nc.tensor.matmul(warm_bank[:], zeros[:, 0:P], zeros[:], start=True, stop=True)
 
         output_tiles = [(mb, piece) for mb in range(M_BLOCKS) for piece in range(PIECES)]
         banks = {}

@@ -10,13 +10,20 @@ PIECE = 512
 PIECES = N // PIECE
 PIECE_COLUMNS = PIECE // 16
 
-WARM_UPS = 7
-
 FLOPS = 2 * K * M * N
 
 
 def tile_gather_matmul_kernel(tc, table, w, u, offs, out):
     nc = tc.nc
+
+    output_tiles = [(mb, piece) for mb in range(M_BLOCKS) for piece in range(PIECES)]
+
+    def block_rows(block):
+        return slice(block * P, (block + 1) * P)
+
+    def piece_columns(piece):
+        return slice(piece * PIECE, (piece + 1) * PIECE)
+
     with (
         tc.tile_pool(name="held", bufs=1) as held,
         tc.psum_pool(name="psum", bufs=1) as psum,
@@ -29,21 +36,13 @@ def tile_gather_matmul_kernel(tc, table, w, u, offs, out):
         table_blocks = []
         for kb in range(K_BLOCKS):
             table_block = held.tile([P, S], BF16, name="table%d" % kb)
-            nc.sync.dma_start(table_block[:], table[kb * P : (kb + 1) * P, :])
+            nc.sync.dma_start(table_block[:], table[block_rows(kb), :])
             table_blocks.append(table_block)
-        factor_blocks = []
-        for mb in range(M_BLOCKS):
-            factor_block = held.tile([P, N], F32, name="factor%d" % mb)
-            nc.sync.dma_start(factor_block[:], u[mb * P : (mb + 1) * P, :])
-            factor_blocks.append(factor_block)
+        factors = {}
+        for mb, piece in output_tiles:
+            factors[mb, piece] = held.tile([P, PIECE], F32, name="factor%d_%d" % (mb, piece))
+            nc.sync.dma_start(factors[mb, piece][:], u[block_rows(mb), piece_columns(piece)])
 
-        zeros = held.tile([P, PIECE], BF16, name="zeros")
-        nc.vector.memset(zeros[:], 0.0)
-        warm_bank = psum.tile([P, PIECE], F32, name="warm_bank")
-        for warm_up in range(WARM_UPS):
-            nc.tensor.matmul(warm_bank[:], zeros[:, 0:P], zeros[:], start=True, stop=True)
-
-        output_tiles = [(mb, piece) for mb in range(M_BLOCKS) for piece in range(PIECES)]
         banks = {}
         for mb, piece in output_tiles:
             banks[mb, piece] = psum.tile([P, PIECE], F32, name="bank%d_%d" % (mb, piece))
@@ -52,7 +51,7 @@ def tile_gather_matmul_kernel(tc, table, w, u, offs, out):
             for mb, piece in output_tiles:
                 nc.tensor.matmul(
                     banks[mb, piece][:],
-                    weights[:, kb, mb * P : (mb + 1) * P],
+                    weights[:, kb, block_rows(mb)],
                     table_blocks[kb][:].indirect(
                         offsets[:, piece * PIECE_COLUMNS : (piece + 1) * PIECE_COLUMNS]
                     ),
@@ -61,9 +60,8 @@ def tile_gather_matmul_kernel(tc, table, w, u, offs, out):
                 )
 
         for mb, piece in output_tiles:
-            columns = slice(piece * PIECE, (piece + 1) * PIECE)
             product = held.tile([P, PIECE], F32, name="product%d_%d" % (mb, piece))
             nc.vector.tensor_tensor(
-                product[:], banks[mb, piece][:], factor_blocks[mb][:, columns], mybir.AluOpType.mult
+                product[:], banks[mb, piece][:], factors[mb, piece][:], mybir.AluOpType.mult
             )
-            nc.scalar.dma_start(out[mb * P : (mb + 1) * P, columns], product[:])
+            nc.scalar.dma_start(out[block_rows(mb), piece_columns(piece)], product[:])

@@ -47,17 +47,18 @@ def tile_gather_matmul_kernel(tc, table, w, u, offs, out):
         for mb, piece in output_tiles:
             banks[mb, piece] = psum.tile([P, PIECE], F32, name="bank%d_%d" % (mb, piece))
 
-        for kb in range(K_BLOCKS):
-            for mb, piece in output_tiles:
-                nc.tensor.matmul(
-                    banks[mb, piece][:],
-                    weights[:, kb, block_rows(mb)],
-                    table_blocks[kb][:].indirect(
-                        offsets[:, piece * PIECE_COLUMNS : (piece + 1) * PIECE_COLUMNS]
-                    ),
-                    start=(kb == 0),
-                    stop=(kb == K_BLOCKS - 1),
-                )
+        for tile_group in (output_tiles[:-1], output_tiles[-1:]):
+            for kb in range(K_BLOCKS):
+                for mb, piece in tile_group:
+                    nc.tensor.matmul(
+                        banks[mb, piece][:],
+                        weights[:, kb, block_rows(mb)],
+                        table_blocks[kb][:].indirect(
+                            offsets[:, piece * PIECE_COLUMNS : (piece + 1) * PIECE_COLUMNS]
+                        ),
+                        start=(kb == 0),
+                        stop=(kb == K_BLOCKS - 1),
+                    )
 
         for mb, piece in output_tiles:
             product = held.tile([P, PIECE], F32, name="product%d_%d" % (mb, piece))

@@ -9,6 +9,8 @@ M_BLOCKS = M // P
 PIECE = 512
 PIECES = N // PIECE
 PIECE_COLUMNS = PIECE // 16
+OUTPUT_TILES = M_BLOCKS * PIECES
+BANKS = OUTPUT_TILES - 1
 
 FLOPS = 2 * K * M * N
 
@@ -26,7 +28,7 @@ def tile_gather_matmul_kernel(tc, table, w, u, offs, out):
 
     with (
         tc.tile_pool(name="held", bufs=1) as held,
-        tc.psum_pool(name="psum", bufs=1) as psum,
+        tc.psum_pool(name="psum", bufs=BANKS) as psum,
     ):
         offsets = held.tile([P, N // 16], U16, name="offsets")
         nc.sync.dma_start(offsets[:], offs)
@@ -43,11 +45,10 @@ def tile_gather_matmul_kernel(tc, table, w, u, offs, out):
             factors[mb, piece] = held.tile([P, PIECE], F32, name="factor%d_%d" % (mb, piece))
             nc.sync.dma_start(factors[mb, piece][:], u[block_rows(mb), piece_columns(piece)])
 
-        banks = {}
-        for mb, piece in output_tiles:
-            banks[mb, piece] = psum.tile([P, PIECE], F32, name="bank%d_%d" % (mb, piece))
-
-        for tile_group in (output_tiles[:-1], output_tiles[-1:]):
+        for tile_group in (output_tiles[:BANKS], output_tiles[BANKS:]):
+            banks = {}
+            for mb, piece in tile_group:
+                banks[mb, piece] = psum.tile([P, PIECE], F32, name="bank", tag="bank")
             for kb in range(K_BLOCKS):
                 for mb, piece in tile_group:
                     nc.tensor.matmul(
@@ -59,10 +60,9 @@ def tile_gather_matmul_kernel(tc, table, w, u, offs, out):
                         start=(kb == 0),
                         stop=(kb == K_BLOCKS - 1),
                     )
-
-        for mb, piece in output_tiles:
-            product = held.tile([P, PIECE], F32, name="product%d_%d" % (mb, piece))
-            nc.vector.tensor_tensor(
-                product[:], banks[mb, piece][:], factors[mb, piece][:], mybir.AluOpType.mult
-            )
-            nc.scalar.dma_start(out[block_rows(mb), piece_columns(piece)], product[:])
+            for mb, piece in tile_group:
+                product = held.tile([P, PIECE], F32, name="product%d_%d" % (mb, piece))
+                nc.vector.tensor_tensor(
+                    product[:], banks[mb, piece][:], factors[mb, piece][:], mybir.AluOpType.mult
+                )
+                nc.scalar.dma_start(out[block_rows(mb), piece_columns(piece)], product[:])

@@ -45,6 +45,7 @@ def tile_gather_matmul_kernel(tc, table, w, u, offs, out):
             factors[mb, piece] = held.tile([P, PIECE], F32, name="factor%d_%d" % (mb, piece))
             nc.sync.dma_start(factors[mb, piece][:], u[block_rows(mb), piece_columns(piece)])
 
+        store_queues = (nc.scalar, nc.sync)
         for tile_group in (output_tiles[:BANKS], output_tiles[BANKS:]):
             banks = {}
             for mb, piece in tile_group:
@@ -65,4 +66,5 @@ def tile_gather_matmul_kernel(tc, table, w, u, offs, out):
                 nc.vector.tensor_tensor(
                     product[:], banks[mb, piece][:], factors[mb, piece][:], mybir.AluOpType.mult
                 )
-                nc.scalar.dma_start(out[block_rows(mb), piece_columns(piece)], product[:])
+                store_queue = store_queues[output_tiles.index((mb, piece)) % len(store_queues)]
+                store_queue.dma_start(out[block_rows(mb), piece_columns(piece)], product[:])

@@ -41,11 +41,17 @@ def tile_gather_matmul_kernel(tc, table, w, u, offs, out):
             nc.sync.dma_start(table_block[:], table[block_rows(kb), :])
             table_blocks.append(table_block)
         factors = {}
-        for mb, piece in output_tiles:
-            factors[mb, piece] = held.tile([P, PIECE], F32, name="factor%d_%d" % (mb, piece))
-            nc.sync.dma_start(factors[mb, piece][:], u[block_rows(mb), piece_columns(piece)])
+        for mb in range(M_BLOCKS):
+            factor_head = held.tile([P, PIECE], F32, name="factor_head%d" % mb)
+            nc.sync.dma_start(factor_head[:], u[block_rows(mb), :PIECE])
+            factor_rest = held.tile([P, N - PIECE], F32, name="factor_rest%d" % mb)
+            nc.sync.dma_start(factor_rest[:], u[block_rows(mb), PIECE:])
+            factors[mb, 0] = factor_head[:]
+            for piece in range(1, PIECES):
+                factors[mb, piece] = factor_rest[:, piece_columns(piece - 1)]
 
         store_queues = (nc.scalar, nc.sync)
+        stores = 0
         for tile_group in (output_tiles[:BANKS], output_tiles[BANKS:]):
             banks = {}
             for mb, piece in tile_group:
@@ -63,8 +69,18 @@ def tile_gather_matmul_kernel(tc, table, w, u, offs, out):
                     )
             for mb, piece in tile_group:
                 product = held.tile([P, PIECE], F32, name="product%d_%d" % (mb, piece))
-                nc.vector.tensor_tensor(
-                    product[:], banks[mb, piece][:], factors[mb, piece][:], mybir.AluOpType.mult
-                )
-                store_queue = store_queues[output_tiles.index((mb, piece)) % len(store_queues)]
-                store_queue.dma_start(out[block_rows(mb), piece_columns(piece)], product[:])
+                parts = 2 if (mb, piece) == output_tiles[-1] else 1
+                width = PIECE // parts
+                for part in range(parts):
+                    columns = slice(part * width, (part + 1) * width)
+                    nc.vector.tensor_tensor(
+                        product[:, columns],
+                        banks[mb, piece][:, columns],
+                        factors[mb, piece][:, columns],
+                        mybir.AluOpType.mult,
+                    )
+                    first = piece * PIECE + part * width
+                    store_queues[stores % len(store_queues)].dma_start(
+                        out[block_rows(mb), first : first + width], product[:, columns]
+                    )
+                    stores += 1

@@ -32,11 +32,14 @@ def tile_gather_matmul_kernel(tc, table, w, u, offs, out):
     ):
         offsets = held.tile([P, N // 16], U16, name="offsets")
         nc.sync.dma_start(offsets[:], offs)
-        weights = held.tile([P, K_BLOCKS, M], BF16, name="weights")
-        nc.scalar.dma_start(weights[:], w.rearrange("(kb p) m -> p kb m", p=P))
 
         table_blocks = []
+        weight_blocks = []
         for kb in range(K_BLOCKS):
+            weight_block = held.tile([P, M], BF16, name="weights%d" % kb)
+            weight_queue = nc.scalar if kb == 0 else nc.sync
+            weight_queue.dma_start(weight_block[:], w[block_rows(kb), :])
+            weight_blocks.append(weight_block)
             table_block = held.tile([P, S], BF16, name="table%d" % kb)
             nc.sync.dma_start(table_block[:], table[block_rows(kb), :])
             table_blocks.append(table_block)
@@ -51,7 +54,6 @@ def tile_gather_matmul_kernel(tc, table, w, u, offs, out):
                 factors[mb, piece] = factor_rest[:, piece_columns(piece - 1)]
 
         store_queues = (nc.scalar, nc.sync)
-        stores = 0
         for tile_group in (output_tiles[:BANKS], output_tiles[BANKS:]):
             banks = {}
             for mb, piece in tile_group:
@@ -60,7 +62,7 @@ def tile_gather_matmul_kernel(tc, table, w, u, offs, out):
                 for mb, piece in tile_group:
                     nc.tensor.matmul(
                         banks[mb, piece][:],
-                        weights[:, kb, block_rows(mb)],
+                        weight_blocks[kb][:, block_rows(mb)],
                         table_blocks[kb][:].indirect(
                             offsets[:, piece * PIECE_COLUMNS : (piece + 1) * PIECE_COLUMNS]
                         ),
@@ -69,18 +71,8 @@ def tile_gather_matmul_kernel(tc, table, w, u, offs, out):
                     )
             for mb, piece in tile_group:
                 product = held.tile([P, PIECE], F32, name="product%d_%d" % (mb, piece))
-                parts = 2 if (mb, piece) == output_tiles[-1] else 1
-                width = PIECE // parts
-                for part in range(parts):
-                    columns = slice(part * width, (part + 1) * width)
-                    nc.vector.tensor_tensor(
-                        product[:, columns],
-                        banks[mb, piece][:, columns],
-                        factors[mb, piece][:, columns],
-                        mybir.AluOpType.mult,
-                    )
-                    first = piece * PIECE + part * width
-                    store_queues[stores % len(store_queues)].dma_start(
-                        out[block_rows(mb), first : first + width], product[:, columns]
-                    )
-                    stores += 1
+                nc.vector.tensor_tensor(
+                    product[:], banks[mb, piece][:], factors[mb, piece], mybir.AluOpType.mult
+                )
+                store_queue = store_queues[output_tiles.index((mb, piece)) % len(store_queues)]
+                store_queue.dma_start(out[block_rows(mb), piece_columns(piece)], product[:])

@@ -37,8 +37,7 @@ def tile_gather_matmul_kernel(tc, table, w, u, offs, out):
         weight_blocks = []
         for kb in range(K_BLOCKS):
             weight_block = held.tile([P, M], BF16, name="weights%d" % kb)
-            weight_queue = nc.scalar if kb == 0 else nc.sync
-            weight_queue.dma_start(weight_block[:], w[block_rows(kb), :])
+            nc.sync.dma_start(weight_block[:], w[block_rows(kb), :])
             weight_blocks.append(weight_block)
             table_block = held.tile([P, S], BF16, name="table%d" % kb)
             nc.sync.dma_start(table_block[:], table[block_rows(kb), :])

@@ -52,7 +52,6 @@ def tile_gather_matmul_kernel(tc, table, w, u, offs, out):
             for piece in range(1, PIECES):
                 factors[mb, piece] = factor_rest[:, piece_columns(piece - 1)]
 
-        store_queues = (nc.scalar, nc.sync)
         for tile_group in (output_tiles[:BANKS], output_tiles[BANKS:]):
             banks = {}
             for mb, piece in tile_group:
@@ -73,5 +72,4 @@ def tile_gather_matmul_kernel(tc, table, w, u, offs, out):
                 nc.vector.tensor_tensor(
                     product[:], banks[mb, piece][:], factors[mb, piece], mybir.AluOpType.mult
                 )
-                store_queue = store_queues[output_tiles.index((mb, piece)) % len(store_queues)]
-                store_queue.dma_start(out[block_rows(mb), piece_columns(piece)], product[:])
+                nc.sync.dma_start(out[block_rows(mb), piece_columns(piece)], product[:])

@@ -69,7 +69,17 @@ def tile_gather_matmul_kernel(tc, table, w, u, offs, out):
                     )
             for mb, piece in tile_group:
                 product = held.tile([P, PIECE], F32, name="product%d_%d" % (mb, piece))
-                nc.vector.tensor_tensor(
-                    product[:], banks[mb, piece][:], factors[mb, piece], mybir.AluOpType.mult
-                )
-                nc.sync.dma_start(out[block_rows(mb), piece_columns(piece)], product[:])
+                parts = 2 if (mb, piece) == output_tiles[-1] else 1
+                width = PIECE // parts
+                for part in range(parts):
+                    columns = slice(part * width, (part + 1) * width)
+                    nc.vector.tensor_tensor(
+                        product[:, columns],
+                        banks[mb, piece][:, columns],
+                        factors[mb, piece][:, columns],
+                        mybir.AluOpType.mult,
+                    )
+                    first = piece * PIECE + part * width
+                    nc.sync.dma_start(
+                        out[block_rows(mb), first : first + width], product[:, columns]
+                    )

@@ -10,6 +10,7 @@ PIECE = 512
 PIECES = N // PIECE
 PIECE_COLUMNS = PIECE // 16
 OUTPUT_TILES = M_BLOCKS * PIECES
+ROW_START = 256
 BANKS = OUTPUT_TILES - 1
 
 FLOPS = 2 * K * M * N
@@ -30,23 +31,29 @@ def tile_gather_matmul_kernel(tc, table, w, u, offs, out):
         tc.tile_pool(name="held", bufs=1) as held,
         tc.psum_pool(name="psum", bufs=BANKS) as psum,
     ):
-        offsets = held.tile([P, N // 16], U16, name="offsets")
+        offsets = held.tile([P, N // 16], U16, name="offsets", align_bytes=ROW_START)
         nc.sync.dma_start(offsets[:], offs)
 
         table_blocks = []
         weight_blocks = []
         for kb in range(K_BLOCKS):
-            weight_block = held.tile([P, M], BF16, name="weights%d" % kb)
+            weight_block = held.tile(
+                [P, M], BF16, name="weights%d" % kb, align_bytes=ROW_START
+            )
             nc.sync.dma_start(weight_block[:], w[block_rows(kb), :])
             weight_blocks.append(weight_block)
-            table_block = held.tile([P, S], BF16, name="table%d" % kb)
+            table_block = held.tile([P, S], BF16, name="table%d" % kb, align_bytes=ROW_START)
             nc.sync.dma_start(table_block[:], table[block_rows(kb), :])
             table_blocks.append(table_block)
         factors = {}
         for mb in range(M_BLOCKS):
-            factor_head = held.tile([P, PIECE], F32, name="factor_head%d" % mb)
+            factor_head = held.tile(
+                [P, PIECE], F32, name="factor_head%d" % mb, align_bytes=ROW_START
+            )
             nc.sync.dma_start(factor_head[:], u[block_rows(mb), :PIECE])
-            factor_rest = held.tile([P, N - PIECE], F32, name="factor_rest%d" % mb)
+            factor_rest = held.tile(
+                [P, N - PIECE], F32, name="factor_rest%d" % mb, align_bytes=ROW_START
+            )
             nc.sync.dma_start(factor_rest[:], u[block_rows(mb), PIECE:])
             factors[mb, 0] = factor_head[:]
             for piece in range(1, PIECES):
@@ -68,7 +75,9 @@ def tile_gather_matmul_kernel(tc, table, w, u, offs, out):
                         stop=(kb == K_BLOCKS - 1),
                     )
             for mb, piece in tile_group:
-                product = held.tile([P, PIECE], F32, name="product%d_%d" % (mb, piece))
+                product = held.tile(
+                    [P, PIECE], F32, name="product%d_%d" % (mb, piece), align_bytes=ROW_START
+                )
                 parts = 2 if (mb, piece) == output_tiles[-1] else 1
                 width = PIECE // parts
                 for part in range(parts):

@@ -34,16 +34,15 @@ def tile_gather_matmul_kernel(tc, table, w, u, offs, out):
         offsets = held.tile([P, N // 16], U16, name="offsets", align_bytes=ROW_START)
         nc.sync.dma_start(offsets[:], offs)
 
+        weights = held.tile([P, K_BLOCKS * M], BF16, name="weights", align_bytes=ROW_START)
+        w_pairs = w.rearrange("(p kb) m -> p (kb m)", kb=K_BLOCKS)
+        table_rows = table.rearrange("(p kb) s -> p kb s", kb=K_BLOCKS)
+        weight_loads = (slice(0, P), slice(P, K_BLOCKS * M))
         table_blocks = []
-        weight_blocks = []
         for kb in range(K_BLOCKS):
-            weight_block = held.tile(
-                [P, M], BF16, name="weights%d" % kb, align_bytes=ROW_START
-            )
-            nc.sync.dma_start(weight_block[:], w[block_rows(kb), :])
-            weight_blocks.append(weight_block)
+            nc.sync.dma_start(weights[:, weight_loads[kb]], w_pairs[:, weight_loads[kb]])
             table_block = held.tile([P, S], BF16, name="table%d" % kb, align_bytes=ROW_START)
-            nc.sync.dma_start(table_block[:], table[block_rows(kb), :])
+            nc.sync.dma_start(table_block[:], table_rows[:, kb, :])
             table_blocks.append(table_block)
         factors = {}
         for mb in range(M_BLOCKS):
@@ -67,7 +66,7 @@ def tile_gather_matmul_kernel(tc, table, w, u, offs, out):
                 for mb, piece in tile_group:
                     nc.tensor.matmul(
                         banks[mb, piece][:],
-                        weight_blocks[kb][:, block_rows(mb)],
+                        weights[:, kb * M + mb * P : kb * M + (mb + 1) * P],
                         table_blocks[kb][:].indirect(
                             offsets[:, piece * PIECE_COLUMNS : (piece + 1) * PIECE_COLUMNS]
                         ),

@@ -31,19 +31,21 @@ def tile_gather_matmul_kernel(tc, table, w, u, offs, out):
         tc.tile_pool(name="held", bufs=1) as held,
         tc.psum_pool(name="psum", bufs=BANKS) as psum,
     ):
+        table_rows = table.rearrange("(p kb) s -> p kb s", kb=K_BLOCKS)
+        table_blocks = [
+            held.tile([P, S], BF16, name="table%d" % kb, align_bytes=ROW_START)
+            for kb in range(K_BLOCKS)
+        ]
+        nc.sync.dma_start(table_blocks[0][:], table_rows[:, 0, :])
+
         offsets = held.tile([P, N // 16], U16, name="offsets", align_bytes=ROW_START)
         nc.sync.dma_start(offsets[:], offs)
 
         weights = held.tile([P, K_BLOCKS * M], BF16, name="weights", align_bytes=ROW_START)
         w_pairs = w.rearrange("(p kb) m -> p (kb m)", kb=K_BLOCKS)
-        table_rows = table.rearrange("(p kb) s -> p kb s", kb=K_BLOCKS)
-        weight_loads = (slice(0, P), slice(P, K_BLOCKS * M))
-        table_blocks = []
-        for kb in range(K_BLOCKS):
-            nc.sync.dma_start(weights[:, weight_loads[kb]], w_pairs[:, weight_loads[kb]])
-            table_block = held.tile([P, S], BF16, name="table%d" % kb, align_bytes=ROW_START)
-            nc.sync.dma_start(table_block[:], table_rows[:, kb, :])
-            table_blocks.append(table_block)
+        for columns in (slice(0, P), slice(P, K_BLOCKS * M)):
+            nc.sync.dma_start(weights[:, columns], w_pairs[:, columns])
+        nc.sync.dma_start(table_blocks[1][:], table_rows[:, 1, :])
         factors = {}
         for mb in range(M_BLOCKS):
             factor_head = held.tile(

import concourse.mybir as mybir

BF16, F32, U16 = mybir.dt.bfloat16, mybir.dt.float32, mybir.dt.uint16

P = 128
K, S, M, N = 256, 4096, 256, 1536
K_BLOCKS = K // P
M_BLOCKS = M // P
PIECE = 512
PIECES = N // PIECE
PIECE_COLUMNS = PIECE // 16
OUTPUT_TILES = M_BLOCKS * PIECES
ROW_START = 256
BANKS = OUTPUT_TILES - 1

FLOPS = 2 * K * M * N


def tile_gather_matmul_kernel(tc, table, w, u, offs, out):
    nc = tc.nc

    output_tiles = [(mb, piece) for mb in range(M_BLOCKS) for piece in range(PIECES)]

    def block_rows(block):
        return slice(block * P, (block + 1) * P)

    def piece_columns(piece):
        return slice(piece * PIECE, (piece + 1) * PIECE)

    with (
        tc.tile_pool(name="held", bufs=1) as held,
        tc.psum_pool(name="psum", bufs=BANKS) as psum,
    ):
        table_rows = table.rearrange("(p kb) s -> p kb s", kb=K_BLOCKS)
        table_blocks = [
            held.tile([P, S], BF16, name="table%d" % kb, align_bytes=ROW_START)
            for kb in range(K_BLOCKS)
        ]
        nc.sync.dma_start(table_blocks[0][:], table_rows[:, 0, :])

        offsets = held.tile([P, N // 16], U16, name="offsets", align_bytes=ROW_START)
        nc.sync.dma_start(offsets[:], offs)

        weights = held.tile([P, K_BLOCKS * M], BF16, name="weights", align_bytes=ROW_START)
        w_pairs = w.rearrange("(p kb) m -> p (kb m)", kb=K_BLOCKS)
        for columns in (slice(0, P), slice(P, K_BLOCKS * M)):
            nc.sync.dma_start(weights[:, columns], w_pairs[:, columns])
        nc.sync.dma_start(table_blocks[1][:], table_rows[:, 1, :])
        factors = {}
        for mb in range(M_BLOCKS):
            factor_head = held.tile(
                [P, PIECE], F32, name="factor_head%d" % mb, align_bytes=ROW_START
            )
            nc.sync.dma_start(factor_head[:], u[block_rows(mb), :PIECE])
            factor_rest = held.tile(
                [P, N - PIECE], F32, name="factor_rest%d" % mb, align_bytes=ROW_START
            )
            nc.sync.dma_start(factor_rest[:], u[block_rows(mb), PIECE:])
            factors[mb, 0] = factor_head[:]
            for piece in range(1, PIECES):
                factors[mb, piece] = factor_rest[:, piece_columns(piece - 1)]

        for tile_group in (output_tiles[:BANKS], output_tiles[BANKS:]):
            banks = {}
            for mb, piece in tile_group:
                banks[mb, piece] = psum.tile([P, PIECE], F32, name="bank", tag="bank")
            for kb in range(K_BLOCKS):
                for mb, piece in tile_group:
                    nc.tensor.matmul(
                        banks[mb, piece][:],
                        weights[:, kb * M + mb * P : kb * M + (mb + 1) * P],
                        table_blocks[kb][:].indirect(
                            offsets[:, piece * PIECE_COLUMNS : (piece + 1) * PIECE_COLUMNS]
                        ),
                        start=(kb == 0),
                        stop=(kb == K_BLOCKS - 1),
                    )
            for mb, piece in tile_group:
                product = held.tile(
                    [P, PIECE], F32, name="product%d_%d" % (mb, piece), align_bytes=ROW_START
                )
                parts = 2 if (mb, piece) == output_tiles[-1] else 1
                width = PIECE // parts
                for part in range(parts):
                    columns = slice(part * width, (part + 1) * width)
                    nc.vector.tensor_tensor(
                        product[:, columns],
                        banks[mb, piece][:, columns],
                        factors[mb, piece][:, columns],
                        mybir.AluOpType.mult,
                    )
                    first = piece * PIECE + part * width
                    nc.sync.dma_start(
                        out[block_rows(mb), first : first + width], product[:, columns]
                    )
